import numpy as np
import ml_dtypes


def mxq(x, axis, fmt="e4m3"):
    dtype, down = {"e4m3": (ml_dtypes.float8_e4m3fn, 7), "e5m2": (ml_dtypes.float8_e5m2, 14)}[fmt]
    v = np.moveaxis(np.asarray(x, np.float32).astype(ml_dtypes.bfloat16).astype(np.float64), axis, -1)
    blocks = v.reshape(v.shape[:-1] + (-1, 32))
    amax = np.abs(blocks).max(-1, keepdims=True)
    byte = np.maximum(np.where(amax > 0, np.frexp(amax)[1] - 1 + 127, 0) - down, 1)
    scale = np.exp2(byte - 127.0)
    codes = (blocks / scale).astype(np.float32).astype(dtype).astype(np.float64)
    return np.moveaxis((codes * scale).reshape(v.shape), -1, axis)


WIDE = False


def mx_kscale(k):
    if not WIDE:
        return np.ones(k)
    levels = np.array([30, -30])
    if k % 512:
        return np.exp2(np.random.permutation(np.resize(levels, k // 32))).repeat(32)
    a = np.empty((k // 512, 16))
    for p in range(k // 512):
        a[p, :8] = np.random.permutation(np.resize(levels, 8))
        for g in range(8):
            far = levels[np.abs(levels - a[p, g]) >= 10]
            a[p, g + 8] = far[np.random.randint(len(far))]
    return np.exp2(a.ravel()).repeat(32)


def f64(x):
    return np.asarray(x).astype(np.float64)


def striped(idx):
    return np.tile(np.asarray(idx).reshape(-1, 16).T, (8, 1)).astype(np.uint16)


def unstriped(offs):
    return offs[:16].T.reshape(-1).astype(np.int64)


E2M1 = np.array([0.0, 0.5, 1.0, 1.5, 2.0, 3.0, 4.0, 6.0, -0.0, -0.5, -1.0, -1.5, -2.0, -3.0, -4.0, -6.0])


def pack_weight(w, fmt):
    k, n = w.shape
    w = f64(np.asarray(w, np.float32).astype(ml_dtypes.bfloat16)).reshape(k // 32, 32, n)
    amax = np.abs(w).max(1)
    if fmt in ("e4m3", "e5m2"):
        byte = np.frexp(amax)[1] - 1 + 127 - (7 if fmt == "e4m3" else 14)
    else:
        mant, ex = np.frexp(amax / 6.0)
        byte = np.where(mant > 0.5, ex, ex - 1) + 127
    byte = np.clip(np.where(amax > 0, byte, 1), 1, 254)
    scaled = (w * np.exp2(127.0 - byte)[:, None, :]).reshape(k, n).astype(np.float32)
    by_word = np.ascontiguousarray(scaled.reshape(k // 512, 128, 4, n).transpose(0, 1, 3, 2))
    if fmt in ("e4m3", "e5m2"):
        words = by_word.astype(ml_dtypes.float8_e4m3fn if fmt == "e4m3" else ml_dtypes.float8_e5m2).view(np.uint8)
    else:
        c = by_word.astype(ml_dtypes.float4_e2m1fn).view(np.uint8) & 0xF
        words = (c[..., 0::2] | (c[..., 1::2] << 4)).reshape(k // 512, 128, 2 * n)
    return np.ascontiguousarray(words), np.ascontiguousarray(byte.astype(np.uint8).reshape(k // 512, 16, n))


def unpack_weight(words, scales, fmt):
    g, _, n = scales.shape
    words = np.ascontiguousarray(words).reshape(g, 128, n, -1)
    if fmt in ("e4m3", "e5m2"):
        vals = words.view(ml_dtypes.float8_e4m3fn if fmt == "e4m3" else ml_dtypes.float8_e5m2).astype(np.float64)
    else:
        nib = np.empty((g, 128, n, 4), np.uint8)
        nib[..., 0::2] = words & 0xF
        nib[..., 1::2] = words >> 4
        vals = E2M1[nib]
    vals = vals * np.repeat(np.exp2(scales.astype(np.float64) - 127.0), 8, axis=1)[..., None]
    return vals.transpose(0, 1, 3, 2).reshape(g * 512, n)


K, T, J, R, C, N, E = 512, 1024, 256, 512, 512, 256, 128


def setup_inputs():
    n = np.random.standard_normal
    idx = np.random.permutation(T)[:J]
    idx2 = np.random.permutation(C)[:J]
    idx3 = np.random.permutation(C)[:J]
    idx4 = np.random.permutation(J)[:E]
    idx5 = np.random.permutation(J)[:E]
    fk = mx_kscale(K)
    fr = mx_kscale(R)
    xtp = pack_weight(n((K, T)) / fk[:, None], "e2m1")
    wp = pack_weight(n((K, R)) * 1 / np.sqrt(K) * fk[:, None] * fr, "e5m2")
    w2p = pack_weight(n((K, R)) * 1 / np.sqrt(K) * fk[:, None] * fr, "e4m3")
    wbp = pack_weight(n((R, N)) * 1 / np.sqrt(R) / fr[:, None], "e4m3")
    wsp = pack_weight(n((K, N)) * 1 / np.sqrt(K) * fk[:, None], "e4m3")
    return {
        "xt_words": xtp[0],
        "xt_scales": xtp[1],
        "w_words": wp[0],
        "w_scales": wp[1],
        "w2_words": w2p[0],
        "w2_scales": w2p[1],
        "wb_words": wbp[0],
        "wb_scales": wbp[1],
        "ws_words": wsp[0],
        "ws_scales": wsp[1],
        "offs": striped(idx),
        "offs2": striped(idx2),
        "offs3": striped(idx3),
        "offs4": striped(idx4),
        "offs5": striped(idx5),
    }


def reference(xt_words, xt_scales, w_words, w_scales, w2_words, w2_scales, wb_words, wb_scales, ws_words, ws_scales, offs, offs2, offs3, offs4, offs5):
    idx = unstriped(offs)
    idx2 = unstriped(offs2)
    idx3 = unstriped(offs3)
    idx4 = unstriped(offs4)
    idx5 = unstriped(offs5)
    xtu = unpack_weight(xt_words, xt_scales, "e2m1")
    wu = unpack_weight(w_words, w_scales, "e5m2")
    w2u = unpack_weight(w2_words, w2_scales, "e4m3")
    wbu = unpack_weight(wb_words, wb_scales, "e4m3")
    wsu = unpack_weight(ws_words, ws_scales, "e4m3")
    xtidxg = xtu[:, idx]
    a = wu.T @ xtidxg
    b = w2u.T @ xtidxg
    pw = np.zeros((R, C))
    pw[:, idx2] = a
    hid = np.maximum(pw[:, idx3], b)
    hidq = mxq(hid, 0, "e5m2")
    p = wbu.T @ hidq + wsu.T @ xtidxg
    y = np.maximum(p[:, idx4], p[:, idx5])
    return y

@@ -1,0 +1,198 @@
+from contextlib import ExitStack
+
+import concourse.mybir as mybir
+
+K, T, J, R, C, N, E = 512, 1024, 256, 512, 512, 256, 128
+FLOPS = 2 * J * (2 * K * R + R * N + K * N)
+
+F32 = mybir.dt.float32
+BF16 = mybir.dt.bfloat16
+I32 = mybir.dt.int32
+U32 = mybir.dt.uint32
+U16 = mybir.dt.uint16
+U8 = mybir.dt.uint8
+E4M3 = mybir.dt.float8_e4m3fn_x4
+E5M2 = mybir.dt.float8_e5m2_x4
+E2M1 = mybir.dt.float4_e2m1fn_x4
+COPY = mybir.ActivationFunctionType.Copy
+MAX = mybir.AluOpType.max
+
+P = 128
+PACK = 4
+HALF = J // 2
+STRIPE = 16
+
+
+def load_scale_rows(queue, plane, scales, quadrants):
+    for q in quadrants:
+        queue.dma_start(out=plane[32 * q : 32 * q + 4, :].bitcast(I32), in_=scales[0, 4 * q : 4 * q + 4, :].bitcast(I32))
+
+
+def load_scale_quadrants(queue, plane, scales, quadrants):
+    for q in quadrants:
+        rows = scales[0, 4 * q : 4 * q + 4, :].bitcast(I32)
+        queue.dma_start(
+            out=plane[32 * q : 32 * q + 32, :].bitcast(I32),
+            in_=rows.unsqueeze(0).to_broadcast([8, 4, rows.shape[1]]),
+        )
+
+
+def load_words(queue, tile, words):
+    queue.dma_start(out=tile[:].bitcast(I32), in_=words[0].rearrange("p n t -> p (n t)").bitcast(I32))
+
+
+def dealt_views(dealt, natural, run):
+    return (
+        dealt.rearrange("p (t c i) -> p c t i", t=PACK, i=run),
+        natural.rearrange("p (c i t) -> p c t i", t=PACK, i=run),
+    )
+
+
+def half_of(offsets, h):
+    cols = HALF // STRIPE
+    return offsets[:, h * cols : (h + 1) * cols]
+
+
+def tile_list_twow_board_skip_bestoftwo_kernel(
+    tc, xt_words, xt_scales, w_words, w_scales, w2_words, w2_scales, wb_words, wb_scales, ws_words, ws_scales,
+    offs, offs2, offs3, offs4, offs5, out,
+):
+    nc = tc.nc
+    with ExitStack() as ctx:
+        lists = ctx.enter_context(tc.tile_pool(name="lists", bufs=1))
+        sb = ctx.enter_context(tc.tile_pool(name="sb", bufs=1))
+        psum = ctx.enter_context(tc.psum_pool(name="psum", bufs=1))
+
+        token_list = lists.tile([P, J // STRIPE], U16, name="token_list")
+        put_list = lists.tile([P, J // STRIPE], U16, name="put_list")
+        read_list = lists.tile([P, J // STRIPE], U16, name="read_list")
+        left_list = lists.tile([P, E // STRIPE], U16, name="left_list")
+        right_list = lists.tile([P, E // STRIPE], U16, name="right_list")
+
+        x_words = sb.tile([P, T], U16, name="x_words", align_bytes=64)
+        x_plane = sb.tile([P, T], U8, name="x_plane", align_bytes=64)
+        w_nat = sb.tile([P, R], U32, name="w_nat", align_bytes=64)
+        w_plane_nat = sb.tile([P, R], U8, name="w_plane_nat", align_bytes=64)
+        w2_nat = sb.tile([P, R], U32, name="w2_nat", align_bytes=64)
+        w2_plane_nat = sb.tile([P, R], U8, name="w2_plane_nat", align_bytes=64)
+        wb_codes = sb.tile([P, N], U32, name="wb_codes", align_bytes=64)
+        ws_codes = sb.tile([P, N], U32, name="ws_codes", align_bytes=64)
+        wb_plane = sb.tile([P, N], U8, name="wb_plane", align_bytes=64)
+        ws_plane = sb.tile([P, N], U8, name="ws_plane", align_bytes=64)
+        boards = [sb.tile([P, C], F32, name="board%d" % t) for t in range(PACK)]
+
+        for board in boards:
+            nc.vector.memset(board[:], 0.0)
+        for plane in (ws_plane, wb_plane):
+            nc.vector.memset(plane[:].bitcast(I32), 0)
+
+        nc.sync.dma_start(token_list[:], offs)
+        nc.scalar.dma_start(out=x_words[:].bitcast(I32), in_=xt_words[0].bitcast(I32))
+        load_scale_quadrants(nc.sync, x_plane, xt_scales, range(4))
+        load_words(nc.scalar, w_nat, w_words)
+        load_words(nc.gpsimd, w2_nat, w2_words)
+        load_scale_quadrants(nc.sync, w_plane_nat, w_scales, range(4))
+        nc.sync.dma_start(put_list[:], offs2)
+        load_scale_quadrants(nc.sync, w2_plane_nat, w2_scales, range(4))
+        nc.sync.dma_start(read_list[:], offs3)
+        load_words(nc.sync, ws_codes, ws_words)
+        load_words(nc.sync, wb_codes, wb_words)
+        nc.sync.dma_start(left_list[:], offs4)
+        nc.sync.dma_start(right_list[:], offs5)
+        load_scale_rows(nc.sync, ws_plane, ws_scales, range(4))
+        load_scale_rows(nc.sync, wb_plane, wb_scales, range(4))
+
+        xg_words = sb.tile([P, J], U16, name="xg_words", align_bytes=64)
+        xg_plane = sb.tile([P, J], U8, name="xg_plane", align_bytes=64)
+        nc.vector.tensor_copy(xg_words[:], x_words[:].indirect(token_list[:]))
+        nc.vector.tensor_copy(xg_plane[:], x_plane[:].indirect(token_list[:]))
+
+        w_codes = sb.tile([P, R], U32, name="w_codes", align_bytes=64)
+        w_plane = sb.tile([P, R], U8, name="w_plane", align_bytes=64)
+        w2_codes = sb.tile([P, R], U32, name="w2_codes", align_bytes=64)
+        w2_plane = sb.tile([P, R], U8, name="w2_plane", align_bytes=64)
+        nc.scalar.copy(*dealt_views(w_codes[:], w_nat[:], 4))
+        nc.scalar.copy(*dealt_views(w2_codes[:], w2_nat[:], 4))
+        dealt, natural = dealt_views(w_plane[:], w_plane_nat[:], 16)
+        for t0 in (0, 2):
+            nc.vector.tensor_copy(dealt[:, :, t0 : t0 + 2, :], natural[:, :, t0 : t0 + 2, :])
+        nc.vector.tensor_copy(*dealt_views(w2_plane[:], w2_plane_nat[:], 16))
+
+        def rows(t):
+            return slice(t * P, (t + 1) * P)
+
+        def slots(h):
+            return slice(h * HALF, (h + 1) * HALF)
+
+        a_psum = {}
+        for t in range(PACK):
+            a_psum[t] = psum.tile([P, J], F32, name="a%d" % t, tag="bank%d" % t)
+            nc.tensor.matmul_mx(
+                out=a_psum[t][:], lhsT=w_codes[:, rows(t)].bitcast(E5M2), lhsT_scale=w_plane[:, rows(t)],
+                rhs=xg_words[:].bitcast(E2M1), rhs_scale=xg_plane[:], start=True, stop=True,
+            )
+        b_psum = []
+        for h in range(2):
+            bank = psum.tile([P, PACK, HALF], F32, name="b%d" % h)
+            b_psum.append(bank)
+            for t in range(PACK):
+                nc.tensor.matmul_mx(
+                    out=bank[:, t, :], lhsT=w2_codes[:, rows(t)].bitcast(E4M3), lhsT_scale=w2_plane[:, rows(t)],
+                    rhs=xg_words[:, slots(h)].bitcast(E2M1), rhs_scale=xg_plane[:, slots(h)], start=True, stop=True,
+                )
+
+        a_sb = [sb.tile([P, J], F32, name="a_sb%d" % t) for t in range(PACK)]
+        for t in (0, 2):
+            nc.scalar.copy(a_sb[t][:], a_psum[t][:])
+            nc.vector.tensor_copy(a_sb[t + 1][:], a_psum[t + 1][:])
+        for t in (0, 2):
+            nc.scalar.activation(boards[t][:].indirect(put_list[:]), a_sb[t][:], COPY)
+            nc.vector.tensor_copy(boards[t + 1][:].indirect(put_list[:]), a_sb[t + 1][:])
+
+        p_psum = {}
+        for h in range(2):
+            for u in range(2):
+                p_psum[h, u] = psum.tile([P, HALF], F32, name="p%d%d" % (h, u), tag="bank%d" % (2 * h + u))
+                nc.tensor.matmul_mx(
+                    out=p_psum[h, u][:], lhsT=ws_codes[:, rows(u)].bitcast(E4M3), lhsT_scale=ws_plane[:, rows(u)],
+                    rhs=xg_words[:, slots(h)].bitcast(E2M1), rhs_scale=xg_plane[:, slots(h)], start=True, stop=False,
+                )
+
+        picked = [sb.tile([P, PACK, HALF], F32, name="picked%d" % h) for h in range(2)]
+        for t, h in ((1, 0), (3, 0), (1, 1)):
+            nc.vector.tensor_copy(picked[h][:, t, :], boards[t][:].indirect(half_of(read_list, h)))
+        for t, h in ((0, 0), (2, 0), (0, 1), (2, 1), (3, 1)):
+            nc.scalar.activation(picked[h][:, t, :], boards[t][:].indirect(half_of(read_list, h)), COPY)
+
+        p_sb = [sb.tile([P, J], F32, name="p_sb%d" % u) for u in range(2)]
+        hid = [sb.tile([P, HALF * PACK], BF16, name="hid%d" % h, align_bytes=64) for h in range(2)]
+        for h in range(2):
+            nc.vector.tensor_tensor(
+                hid[h][:].rearrange("p (c i t) -> p c t i", t=PACK, i=4),
+                picked[h][:].rearrange("p t (c i) -> p c t i", i=4),
+                b_psum[h][:].rearrange("p t (c i) -> p c t i", i=4),
+                MAX,
+            )
+        for h in range(2):
+            hid_codes = sb.tile([P, HALF], U32, name="hid_codes%d" % h, align_bytes=64)
+            hid_plane = sb.tile([P, HALF], U8, name="hid_plane%d" % h, align_bytes=64)
+            nc.vector.quantize_mx(out=hid_codes[:].bitcast(E5M2), scales=hid_plane[:], in_=hid[h][:])
+            for u in range(2):
+                nc.tensor.matmul_mx(
+                    out=p_psum[h, u][:], lhsT=wb_codes[:, rows(u)].bitcast(E4M3), lhsT_scale=wb_plane[:, rows(u)],
+                    rhs=hid_codes[:].bitcast(E5M2), rhs_scale=hid_plane[:], start=False, stop=True,
+                )
+        for h in range(2):
+            nc.vector.tensor_copy(p_sb[0][:, slots(h)], p_psum[h, 0][:])
+            nc.scalar.copy(p_sb[1][:, slots(h)], p_psum[h, 1][:])
+
+        left = sb.tile([P, 2, E], F32, name="left")
+        right = sb.tile([P, 2, E], F32, name="right")
+        best = sb.tile([P, 2, E], F32, name="best")
+        nc.vector.tensor_copy(left[:, 0, :], p_sb[0][:].indirect(left_list[:]))
+        nc.vector.tensor_copy(right[:, 0, :], p_sb[0][:].indirect(right_list[:]))
+        nc.scalar.activation(left[:, 1, :], p_sb[1][:].indirect(left_list[:]), COPY)
+        nc.scalar.activation(right[:, 1, :], p_sb[1][:].indirect(right_list[:]), COPY)
+        for u, queue in ((0, nc.sync), (1, nc.scalar)):
+            nc.vector.tensor_tensor(best[:, u, :], left[:, u, :], right[:, u, :], MAX)
+            queue.dma_start(out=out[rows(u), :], in_=best[:, u, :])

@@ -72,7 +72,7 @@ def tile_list_twow_board_skip_bestoftwo_kernel(
         x_words = sb.tile([P, T], U16, name="x_words", align_bytes=64)
         x_plane = sb.tile([P, T], U8, name="x_plane", align_bytes=64)
         w_nat = sb.tile([P, R], U32, name="w_nat", align_bytes=64)
-        w_plane_nat = sb.tile([P, R], U8, name="w_plane_nat", align_bytes=64)
+        w_plane_nat = sb.tile([P, R], U8, name="w_plane_nat", tag="w_plane_then_w2", align_bytes=64)
         w2_nat = sb.tile([P, R], U32, name="w2_nat", align_bytes=64)
         w2_plane_nat = sb.tile([P, R], U8, name="w2_plane_nat", align_bytes=64)
         wb_codes = sb.tile([P, N], U32, name="wb_codes", align_bytes=64)
@@ -81,19 +81,22 @@ def tile_list_twow_board_skip_bestoftwo_kernel(
         ws_plane = sb.tile([P, N], U8, name="ws_plane", align_bytes=64)
         boards = [sb.tile([P, C], F32, name="board%d" % t) for t in range(PACK)]
 
+        for plane in (w_plane_nat, w2_plane_nat):
+            nc.vector.memset(plane[:].bitcast(I32), 0)
         for board in boards:
             nc.vector.memset(board[:], 0.0)
         for plane in (ws_plane, wb_plane):
             nc.vector.memset(plane[:].bitcast(I32), 0)
 
         nc.sync.dma_start(token_list[:], offs)
-        nc.scalar.dma_start(out=x_words[:].bitcast(I32), in_=xt_words[0].bitcast(I32))
         load_scale_quadrants(nc.sync, x_plane, xt_scales, range(4))
-        load_words(nc.scalar, w_nat, w_words)
-        load_words(nc.gpsimd, w2_nat, w2_words)
-        load_scale_quadrants(nc.sync, w_plane_nat, w_scales, range(4))
+        load_scale_rows(nc.sync, w_plane_nat, w_scales, range(1))
+        nc.sync.dma_start(out=x_words[:].bitcast(I32), in_=xt_words[0].bitcast(I32))
+        load_words(nc.sync, w_nat, w_words)
+        load_scale_rows(nc.sync, w_plane_nat, w_scales, range(1, 4))
+        load_words(nc.sync, w2_nat, w2_words)
+        load_scale_rows(nc.sync, w2_plane_nat, w2_scales, range(4))
         nc.sync.dma_start(put_list[:], offs2)
-        load_scale_quadrants(nc.sync, w2_plane_nat, w2_scales, range(4))
         nc.sync.dma_start(read_list[:], offs3)
         load_words(nc.sync, ws_codes, ws_words)
         load_words(nc.sync, wb_codes, wb_words)
@@ -104,19 +107,19 @@ def tile_list_twow_board_skip_bestoftwo_kernel(
 
         xg_words = sb.tile([P, J], U16, name="xg_words", align_bytes=64)
         xg_plane = sb.tile([P, J], U8, name="xg_plane", align_bytes=64)
-        nc.vector.tensor_copy(xg_words[:], x_words[:].indirect(token_list[:]))
         nc.vector.tensor_copy(xg_plane[:], x_plane[:].indirect(token_list[:]))
+        nc.vector.tensor_copy(xg_words[:], x_words[:].indirect(token_list[:]))
 
         w_codes = sb.tile([P, R], U32, name="w_codes", align_bytes=64)
-        w_plane = sb.tile([P, R], U8, name="w_plane", align_bytes=64)
-        w2_codes = sb.tile([P, R], U32, name="w2_codes", align_bytes=64)
-        w2_plane = sb.tile([P, R], U8, name="w2_plane", align_bytes=64)
-        nc.scalar.copy(*dealt_views(w_codes[:], w_nat[:], 4))
-        nc.scalar.copy(*dealt_views(w2_codes[:], w2_nat[:], 4))
+        w_plane = sb.tile([P, R], U8, name="w_plane", tag="dealt_plane", align_bytes=64)
+        dealt, natural = dealt_views(w_codes[:], w_nat[:], 4)
+        for t0 in (0, 2):
+            nc.scalar.copy(dealt[:, :, t0 : t0 + 2, :], natural[:, :, t0 : t0 + 2, :])
         dealt, natural = dealt_views(w_plane[:], w_plane_nat[:], 16)
         for t0 in (0, 2):
             nc.vector.tensor_copy(dealt[:, :, t0 : t0 + 2, :], natural[:, :, t0 : t0 + 2, :])
-        nc.vector.tensor_copy(*dealt_views(w2_plane[:], w2_plane_nat[:], 16))
+        w2_codes = sb.tile([P, R], U32, name="w2_codes", tag="w_plane_then_w2", align_bytes=64)
+        nc.vector.tensor_copy(*dealt_views(w2_codes[:].bitcast(I32), w2_nat[:].bitcast(I32), 4))
 
         def rows(t):
             return slice(t * P, (t + 1) * P)
@@ -131,6 +134,13 @@ def tile_list_twow_board_skip_bestoftwo_kernel(
                 out=a_psum[t][:], lhsT=w_codes[:, rows(t)].bitcast(E5M2), lhsT_scale=w_plane[:, rows(t)],
                 rhs=xg_words[:].bitcast(E2M1), rhs_scale=xg_plane[:], start=True, stop=True,
             )
+        a_sb = [sb.tile([P, J], F32, name="a_sb%d" % t) for t in range(PACK)]
+        for t in (0, 2):
+            nc.scalar.copy(a_sb[t][:], a_psum[t][:])
+            nc.vector.tensor_copy(a_sb[t + 1][:], a_psum[t + 1][:])
+
+        w2_plane = sb.tile([P, R], U8, name="w2_plane", tag="dealt_plane", align_bytes=64)
+        nc.vector.tensor_copy(*dealt_views(w2_plane[:], w2_plane_nat[:], 16))
         b_psum = []
         for h in range(2):
             bank = psum.tile([P, PACK, HALF], F32, name="b%d" % h)
@@ -141,10 +151,6 @@ def tile_list_twow_board_skip_bestoftwo_kernel(
                     rhs=xg_words[:, slots(h)].bitcast(E2M1), rhs_scale=xg_plane[:, slots(h)], start=True, stop=True,
                 )
 
-        a_sb = [sb.tile([P, J], F32, name="a_sb%d" % t) for t in range(PACK)]
-        for t in (0, 2):
-            nc.scalar.copy(a_sb[t][:], a_psum[t][:])
-            nc.vector.tensor_copy(a_sb[t + 1][:], a_psum[t + 1][:])
         for t in (0, 2):
             nc.scalar.activation(boards[t][:].indirect(put_list[:]), a_sb[t][:], COPY)
             nc.vector.tensor_copy(boards[t + 1][:].indirect(put_list[:]), a_sb[t + 1][:])
@@ -168,9 +174,9 @@ def tile_list_twow_board_skip_bestoftwo_kernel(
         hid = [sb.tile([P, HALF * PACK], BF16, name="hid%d" % h, align_bytes=64) for h in range(2)]
         for h in range(2):
             nc.vector.tensor_tensor(
-                hid[h][:].rearrange("p (c i t) -> p c t i", t=PACK, i=4),
-                picked[h][:].rearrange("p t (c i) -> p c t i", i=4),
-                b_psum[h][:].rearrange("p t (c i) -> p c t i", i=4),
+                hid[h][:].rearrange("p (c i t) -> p c t i", t=PACK, i=2),
+                picked[h][:].rearrange("p t (c i) -> p c t i", i=2),
+                b_psum[h][:].rearrange("p t (c i) -> p c t i", i=2),
                 MAX,
             )
         for h in range(2):
@@ -189,10 +195,9 @@ def tile_list_twow_board_skip_bestoftwo_kernel(
         left = sb.tile([P, 2, E], F32, name="left")
         right = sb.tile([P, 2, E], F32, name="right")
         best = sb.tile([P, 2, E], F32, name="best")
-        nc.vector.tensor_copy(left[:, 0, :], p_sb[0][:].indirect(left_list[:]))
-        nc.vector.tensor_copy(right[:, 0, :], p_sb[0][:].indirect(right_list[:]))
-        nc.scalar.activation(left[:, 1, :], p_sb[1][:].indirect(left_list[:]), COPY)
-        nc.scalar.activation(right[:, 1, :], p_sb[1][:].indirect(right_list[:]), COPY)
+        for u in range(2):
+            nc.vector.tensor_copy(left[:, u, :], p_sb[u][:].indirect(left_list[:]))
+            nc.scalar.activation(right[:, u, :], p_sb[u][:].indirect(right_list[:]), COPY)
         for u, queue in ((0, nc.sync), (1, nc.scalar)):
             nc.vector.tensor_tensor(best[:, u, :], left[:, u, :], right[:, u, :], MAX)
             queue.dma_start(out=out[rows(u), :], in_=best[:, u, :])

@@ -116,8 +116,8 @@ def tile_list_twow_board_skip_bestoftwo_kernel(
         for t0 in (0, 2):
             nc.scalar.copy(dealt[:, :, t0 : t0 + 2, :], natural[:, :, t0 : t0 + 2, :])
         dealt, natural = dealt_views(w_plane[:], w_plane_nat[:], 16)
-        for t0 in (0, 2):
-            nc.vector.tensor_copy(dealt[:, :, t0 : t0 + 2, :], natural[:, :, t0 : t0 + 2, :])
+        for t0, t1 in ((0, 1), (1, 2), (2, 4)):
+            nc.vector.tensor_copy(dealt[:, :, t0:t1, :], natural[:, :, t0:t1, :])
         w2_codes = sb.tile([P, R], U32, name="w2_codes", tag="w_plane_then_w2", align_bytes=64)
         nc.vector.tensor_copy(*dealt_views(w2_codes[:].bitcast(I32), w2_nat[:].bitcast(I32), 4))
 
@@ -198,6 +198,6 @@ def tile_list_twow_board_skip_bestoftwo_kernel(
         for u in range(2):
             nc.vector.tensor_copy(left[:, u, :], p_sb[u][:].indirect(left_list[:]))
             nc.scalar.activation(right[:, u, :], p_sb[u][:].indirect(right_list[:]), COPY)
-        for u, queue in ((0, nc.sync), (1, nc.scalar)):
+        for u in range(2):
             nc.vector.tensor_tensor(best[:, u, :], left[:, u, :], right[:, u, :], MAX)
-            queue.dma_start(out=out[rows(u), :], in_=best[:, u, :])
+            nc.sync.dma_start(out=out[rows(u), :], in_=best[:, u, :])

from contextlib import ExitStack

import concourse.mybir as mybir

K, T, J, R, C, N, E = 512, 1024, 256, 512, 512, 256, 128
FLOPS = 2 * J * (2 * K * R + R * N + K * N)

F32 = mybir.dt.float32
BF16 = mybir.dt.bfloat16
I32 = mybir.dt.int32
U32 = mybir.dt.uint32
U16 = mybir.dt.uint16
U8 = mybir.dt.uint8
E4M3 = mybir.dt.float8_e4m3fn_x4
E5M2 = mybir.dt.float8_e5m2_x4
E2M1 = mybir.dt.float4_e2m1fn_x4
COPY = mybir.ActivationFunctionType.Copy
MAX = mybir.AluOpType.max

P = 128
PACK = 4
HALF = J // 2
STRIPE = 16


def load_scale_rows(queue, plane, scales, quadrants):
    for q in quadrants:
        queue.dma_start(out=plane[32 * q : 32 * q + 4, :].bitcast(I32), in_=scales[0, 4 * q : 4 * q + 4, :].bitcast(I32))


def load_scale_quadrants(queue, plane, scales, quadrants):
    for q in quadrants:
        rows = scales[0, 4 * q : 4 * q + 4, :].bitcast(I32)
        queue.dma_start(
            out=plane[32 * q : 32 * q + 32, :].bitcast(I32),
            in_=rows.unsqueeze(0).to_broadcast([8, 4, rows.shape[1]]),
        )


def load_words(queue, tile, words):
    queue.dma_start(out=tile[:].bitcast(I32), in_=words[0].rearrange("p n t -> p (n t)").bitcast(I32))


def dealt_views(dealt, natural, run):
    return (
        dealt.rearrange("p (t c i) -> p c t i", t=PACK, i=run),
        natural.rearrange("p (c i t) -> p c t i", t=PACK, i=run),
    )


def half_of(offsets, h):
    cols = HALF // STRIPE
    return offsets[:, h * cols : (h + 1) * cols]


def tile_list_twow_board_skip_bestoftwo_kernel(
    tc, xt_words, xt_scales, w_words, w_scales, w2_words, w2_scales, wb_words, wb_scales, ws_words, ws_scales,
    offs, offs2, offs3, offs4, offs5, out,
):
    nc = tc.nc
    with ExitStack() as ctx:
        lists = ctx.enter_context(tc.tile_pool(name="lists", bufs=1))
        sb = ctx.enter_context(tc.tile_pool(name="sb", bufs=1))
        psum = ctx.enter_context(tc.psum_pool(name="psum", bufs=1))

        token_list = lists.tile([P, J // STRIPE], U16, name="token_list")
        put_list = lists.tile([P, J // STRIPE], U16, name="put_list")
        read_list = lists.tile([P, J // STRIPE], U16, name="read_list")
        left_list = lists.tile([P, E // STRIPE], U16, name="left_list")
        right_list = lists.tile([P, E // STRIPE], U16, name="right_list")

        x_words = sb.tile([P, T], U16, name="x_words", align_bytes=64)
        x_plane = sb.tile([P, T], U8, name="x_plane", align_bytes=64)
        w_nat = sb.tile([P, R], U32, name="w_nat", align_bytes=64)
        w_plane_nat = sb.tile([P, R], U8, name="w_plane_nat", tag="w_plane_then_w2", align_bytes=64)
        w2_nat = sb.tile([P, R], U32, name="w2_nat", align_bytes=64)
        w2_plane_nat = sb.tile([P, R], U8, name="w2_plane_nat", align_bytes=64)
        wb_codes = sb.tile([P, N], U32, name="wb_codes", align_bytes=64)
        ws_codes = sb.tile([P, N], U32, name="ws_codes", align_bytes=64)
        wb_plane = sb.tile([P, N], U8, name="wb_plane", align_bytes=64)
        ws_plane = sb.tile([P, N], U8, name="ws_plane", align_bytes=64)
        boards = [sb.tile([P, C], F32, name="board%d" % t) for t in range(PACK)]

        for plane in (w_plane_nat, w2_plane_nat):
            nc.vector.memset(plane[:].bitcast(I32), 0)
        for board in boards:
            nc.vector.memset(board[:], 0.0)
        for plane in (ws_plane, wb_plane):
            nc.vector.memset(plane[:].bitcast(I32), 0)

        nc.sync.dma_start(token_list[:], offs)
        load_scale_quadrants(nc.sync, x_plane, xt_scales, range(4))
        load_scale_rows(nc.sync, w_plane_nat, w_scales, range(1))
        nc.sync.dma_start(out=x_words[:].bitcast(I32), in_=xt_words[0].bitcast(I32))
        load_words(nc.sync, w_nat, w_words)
        load_scale_rows(nc.sync, w_plane_nat, w_scales, range(1, 4))
        load_words(nc.sync, w2_nat, w2_words)
        load_scale_rows(nc.sync, w2_plane_nat, w2_scales, range(4))
        nc.sync.dma_start(put_list[:], offs2)
        nc.sync.dma_start(read_list[:], offs3)
        load_words(nc.sync, ws_codes, ws_words)
        load_words(nc.sync, wb_codes, wb_words)
        nc.sync.dma_start(left_list[:], offs4)
        nc.sync.dma_start(right_list[:], offs5)
        load_scale_rows(nc.sync, ws_plane, ws_scales, range(4))
        load_scale_rows(nc.sync, wb_plane, wb_scales, range(4))

        xg_words = sb.tile([P, J], U16, name="xg_words", align_bytes=64)
        xg_plane = sb.tile([P, J], U8, name="xg_plane", align_bytes=64)
        nc.vector.tensor_copy(xg_plane[:], x_plane[:].indirect(token_list[:]))
        nc.vector.tensor_copy(xg_words[:], x_words[:].indirect(token_list[:]))

        w_codes = sb.tile([P, R], U32, name="w_codes", align_bytes=64)
        w_plane = sb.tile([P, R], U8, name="w_plane", tag="dealt_plane", align_bytes=64)
        dealt, natural = dealt_views(w_codes[:], w_nat[:], 4)
        for t0 in (0, 2):
            nc.scalar.copy(dealt[:, :, t0 : t0 + 2, :], natural[:, :, t0 : t0 + 2, :])
        dealt, natural = dealt_views(w_plane[:], w_plane_nat[:], 16)
        for t0, t1 in ((0, 1), (1, 2), (2, 4)):
            nc.vector.tensor_copy(dealt[:, :, t0:t1, :], natural[:, :, t0:t1, :])
        w2_codes = sb.tile([P, R], U32, name="w2_codes", tag="w_plane_then_w2", align_bytes=64)
        nc.vector.tensor_copy(*dealt_views(w2_codes[:].bitcast(I32), w2_nat[:].bitcast(I32), 4))

        def rows(t):
            return slice(t * P, (t + 1) * P)

        def slots(h):
            return slice(h * HALF, (h + 1) * HALF)

        a_psum = {}
        for t in range(PACK):
            a_psum[t] = psum.tile([P, J], F32, name="a%d" % t, tag="bank%d" % t)
            nc.tensor.matmul_mx(
                out=a_psum[t][:], lhsT=w_codes[:, rows(t)].bitcast(E5M2), lhsT_scale=w_plane[:, rows(t)],
                rhs=xg_words[:].bitcast(E2M1), rhs_scale=xg_plane[:], start=True, stop=True,
            )
        a_sb = [sb.tile([P, J], F32, name="a_sb%d" % t) for t in range(PACK)]
        for t in (0, 2):
            nc.scalar.copy(a_sb[t][:], a_psum[t][:])
            nc.vector.tensor_copy(a_sb[t + 1][:], a_psum[t + 1][:])

        w2_plane = sb.tile([P, R], U8, name="w2_plane", tag="dealt_plane", align_bytes=64)
        nc.vector.tensor_copy(*dealt_views(w2_plane[:], w2_plane_nat[:], 16))
        b_psum = []
        for h in range(2):
            bank = psum.tile([P, PACK, HALF], F32, name="b%d" % h)
            b_psum.append(bank)
            for t in range(PACK):
                nc.tensor.matmul_mx(
                    out=bank[:, t, :], lhsT=w2_codes[:, rows(t)].bitcast(E4M3), lhsT_scale=w2_plane[:, rows(t)],
                    rhs=xg_words[:, slots(h)].bitcast(E2M1), rhs_scale=xg_plane[:, slots(h)], start=True, stop=True,
                )

        for t in (0, 2):
            nc.scalar.activation(boards[t][:].indirect(put_list[:]), a_sb[t][:], COPY)
            nc.vector.tensor_copy(boards[t + 1][:].indirect(put_list[:]), a_sb[t + 1][:])

        p_psum = {}
        for h in range(2):
            for u in range(2):
                p_psum[h, u] = psum.tile([P, HALF], F32, name="p%d%d" % (h, u), tag="bank%d" % (2 * h + u))
                nc.tensor.matmul_mx(
                    out=p_psum[h, u][:], lhsT=ws_codes[:, rows(u)].bitcast(E4M3), lhsT_scale=ws_plane[:, rows(u)],
                    rhs=xg_words[:, slots(h)].bitcast(E2M1), rhs_scale=xg_plane[:, slots(h)], start=True, stop=False,
                )

        picked = [sb.tile([P, PACK, HALF], F32, name="picked%d" % h) for h in range(2)]
        for t, h in ((1, 0), (3, 0), (1, 1)):
            nc.vector.tensor_copy(picked[h][:, t, :], boards[t][:].indirect(half_of(read_list, h)))
        for t, h in ((0, 0), (2, 0), (0, 1), (2, 1), (3, 1)):
            nc.scalar.activation(picked[h][:, t, :], boards[t][:].indirect(half_of(read_list, h)), COPY)

        p_sb = [sb.tile([P, J], F32, name="p_sb%d" % u) for u in range(2)]
        hid = [sb.tile([P, HALF * PACK], BF16, name="hid%d" % h, align_bytes=64) for h in range(2)]
        for h in range(2):
            nc.vector.tensor_tensor(
                hid[h][:].rearrange("p (c i t) -> p c t i", t=PACK, i=2),
                picked[h][:].rearrange("p t (c i) -> p c t i", i=2),
                b_psum[h][:].rearrange("p t (c i) -> p c t i", i=2),
                MAX,
            )
        for h in range(2):
            hid_codes = sb.tile([P, HALF], U32, name="hid_codes%d" % h, align_bytes=64)
            hid_plane = sb.tile([P, HALF], U8, name="hid_plane%d" % h, align_bytes=64)
            nc.vector.quantize_mx(out=hid_codes[:].bitcast(E5M2), scales=hid_plane[:], in_=hid[h][:])
            for u in range(2):
                nc.tensor.matmul_mx(
                    out=p_psum[h, u][:], lhsT=wb_codes[:, rows(u)].bitcast(E4M3), lhsT_scale=wb_plane[:, rows(u)],
                    rhs=hid_codes[:].bitcast(E5M2), rhs_scale=hid_plane[:], start=False, stop=True,
                )
        for h in range(2):
            nc.vector.tensor_copy(p_sb[0][:, slots(h)], p_psum[h, 0][:])
            nc.scalar.copy(p_sb[1][:, slots(h)], p_psum[h, 1][:])

        left = sb.tile([P, 2, E], F32, name="left")
        right = sb.tile([P, 2, E], F32, name="right")
        best = sb.tile([P, 2, E], F32, name="best")
        for u in range(2):
            nc.vector.tensor_copy(left[:, u, :], p_sb[u][:].indirect(left_list[:]))
            nc.scalar.activation(right[:, u, :], p_sb[u][:].indirect(right_list[:]), COPY)
        for u in range(2):
            nc.vector.tensor_tensor(best[:, u, :], left[:, u, :], right[:, u, :], MAX)
            nc.sync.dma_start(out=out[rows(u), :], in_=best[:, u, :])
